import numpy as np
import ml_dtypes


def mxq(x, axis, fmt="e4m3"):
    dtype, down = {"e4m3": (ml_dtypes.float8_e4m3fn, 7), "e5m2": (ml_dtypes.float8_e5m2, 14)}[fmt]
    v = np.moveaxis(np.asarray(x, np.float32).astype(ml_dtypes.bfloat16).astype(np.float64), axis, -1)
    blocks = v.reshape(v.shape[:-1] + (-1, 32))
    amax = np.abs(blocks).max(-1, keepdims=True)
    byte = np.maximum(np.where(amax > 0, np.frexp(amax)[1] - 1 + 127, 0) - down, 1)
    scale = np.exp2(byte - 127.0)
    codes = (blocks / scale).astype(np.float32).astype(dtype).astype(np.float64)
    return np.moveaxis((codes * scale).reshape(v.shape), -1, axis)


WIDE = False


def mx_kscale(k):
    if not WIDE:
        return np.ones(k)
    levels = np.array([10, -10, 5, -5, 0])
    if k % 512:
        return np.exp2(np.random.permutation(np.resize(levels, k // 32))).repeat(32)
    a = np.empty((k // 512, 16))
    for p in range(k // 512):
        a[p, :8] = np.random.permutation(np.resize(levels, 8))
        for g in range(8):
            far = levels[np.abs(levels - a[p, g]) >= 10]
            a[p, g + 8] = far[np.random.randint(len(far))]
    return np.exp2(a.ravel()).repeat(32)


def f64(x):
    return np.asarray(x).astype(np.float64)


def striped(idx):
    return np.tile(np.asarray(idx).reshape(-1, 16).T, (8, 1)).astype(np.uint16)


def unstriped(offs):
    return offs[:16].T.reshape(-1).astype(np.int64)


E2M1 = np.array([0.0, 0.5, 1.0, 1.5, 2.0, 3.0, 4.0, 6.0, -0.0, -0.5, -1.0, -1.5, -2.0, -3.0, -4.0, -6.0])


def pack_weight(w, fmt):
    k, n = w.shape
    w = f64(np.asarray(w, np.float32).astype(ml_dtypes.bfloat16)).reshape(k // 32, 32, n)
    amax = np.abs(w).max(1)
    if fmt == "e4m3":
        byte = np.frexp(amax)[1] - 1 + 127 - 7
    else:
        mant, ex = np.frexp(amax / 6.0)
        byte = np.where(mant > 0.5, ex, ex - 1) + 127
    byte = np.clip(np.where(amax > 0, byte, 1), 1, 254)
    scaled = (w * np.exp2(127.0 - byte)[:, None, :]).reshape(k, n).astype(np.float32)
    by_word = np.ascontiguousarray(scaled.reshape(k // 512, 128, 4, n).transpose(0, 1, 3, 2))
    if fmt == "e4m3":
        words = by_word.astype(ml_dtypes.float8_e4m3fn).view(np.uint8)
    else:
        c = by_word.astype(ml_dtypes.float4_e2m1fn).view(np.uint8) & 0xF
        words = (c[..., 0::2] | (c[..., 1::2] << 4)).reshape(k // 512, 128, 2 * n)
    return np.ascontiguousarray(words), np.ascontiguousarray(byte.astype(np.uint8).reshape(k // 512, 16, n))


def unpack_weight(words, scales, fmt):
    g, _, n = scales.shape
    words = np.ascontiguousarray(words).reshape(g, 128, n, -1)
    if fmt == "e4m3":
        vals = words.view(ml_dtypes.float8_e4m3fn).astype(np.float64)
    else:
        nib = np.empty((g, 128, n, 4), np.uint8)
        nib[..., 0::2] = words & 0xF
        nib[..., 1::2] = words >> 4
        vals = E2M1[nib]
    vals = vals * np.repeat(np.exp2(scales.astype(np.float64) - 127.0), 8, axis=1)[..., None]
    return vals.transpose(0, 1, 3, 2).reshape(g * 512, n)


def sigmoid(v):
    return 1.0 / (1.0 + np.exp(-v))


D, E, T, I, Q = 512, 512, 2048, 512, 128


def setup_inputs():
    n = np.random.standard_normal
    idx = np.random.permutation(T)[:I]
    fd = mx_kscale(D)
    fe = mx_kscale(E)
    keysp = pack_weight(n((D, T)) / fd[:, None], "e4m3")
    valsp = pack_weight(n((E, T)) / fe[:, None], "e4m3")
    return {
        "query": (n((D, Q)) * 1.0 / np.sqrt(D) * fd[:, None]).astype(np.float32),
        "query2": (n((D, Q)) * 1.0 / np.sqrt(D) * fd[:, None]).astype(np.float32),
        "keys_words": keysp[0],
        "keys_scales": keysp[1],
        "th": (np.random.uniform(0.3, 1.5, (Q, 1))).astype(np.float32),
        "gout": (n((E, Q)) * 1 / np.sqrt(E) * fe[:, None]).astype(np.float32),
        "vals_words": valsp[0],
        "vals_scales": valsp[1],
        "size": (np.random.uniform(0.5, 2.0, (1, I))).astype(np.float32),
        "old": (0.5 * n((Q, T))).astype(np.float32),
        "offs": striped(idx),
    }


def reference(query, query2, keys_words, keys_scales, th, gout, vals_words, vals_scales, size, old, offs):
    idx = unstriped(offs)
    keysu = unpack_weight(keys_words, keys_scales, "e4m3")
    valsu = unpack_weight(vals_words, vals_scales, "e4m3")
    queryq = mxq(f64(query), 0, "e4m3")
    keysidxg = keysu[:, idx]
    a = queryq.T @ keysidxg
    query2q = mxq(f64(query2), 0, "e4m3")
    b = query2q.T @ keysidxg
    ua = sigmoid(a - f64(th))
    ub = sigmoid(b - f64(th))
    p = 1.0 - (1.0 - ua) * (1.0 - ub)
    z = np.sum(p, axis=1, keepdims=True)
    goutq = mxq(f64(gout), 0, "e4m3")
    valsidxg = valsu[:, idx]
    c0 = goutq.T @ valsidxg
    dz = np.sum(c0 * p * f64(size) / np.square(z) * (-1.0), axis=1, keepdims=True)
    dp = c0 / z * f64(size) + dz
    dua = dp * (-1.0) * (1.0 - ub) * (-1.0)
    da = dua * ua * (1.0 - ua)
    gs = da * 512.0
    gf = np.zeros((Q, T))
    gf[:, idx] = gs
    y = f64(old) + gf
    return y

@@ -1,0 +1,171 @@
+from contextlib import ExitStack
+
+import concourse.mybir as mybir
+from concourse.masks import make_identity
+
+F32 = mybir.dt.float32
+BF16 = mybir.dt.bfloat16
+I32 = mybir.dt.int32
+U32 = mybir.dt.uint32
+U16 = mybir.dt.uint16
+U8 = mybir.dt.uint8
+FP8X4 = mybir.dt.float8_e4m3fn_x4
+ALU = mybir.AluOpType
+ACT = mybir.ActivationFunctionType
+
+P = 128
+PACK = 4
+T, SLOTS, Q = 2048, 512, 128
+HALF = SLOTS // 2
+FLOPS = 3 * 2 * 512 * Q * SLOTS
+OUT_WIDTHS = [256, 512, 512, 512, 256]
+
+
+def tile_attend_beitherquestion_s_kernel(tc, query, query2, keys_words, keys_scales, th, gout,
+                                          vals_words, vals_scales, size, old, offs, out):
+    nc = tc.nc
+    with ExitStack() as ctx:
+        sb = ctx.enter_context(tc.tile_pool(name="sb", bufs=1))
+        ps = ctx.enter_context(tc.psum_pool(name="ps", bufs=1))
+
+        offsets = sb.tile([P, SLOTS // 16], U16, name="offsets")
+        nc.sync.dma_start(offsets[:], offs)
+
+        def load_scale_rows(name, scales, row0):
+            plane = sb.tile([P, T], U8, name=name, align_bytes=64)
+            nc.vector.memset(plane[:].bitcast(I32), 0)
+            for quad in range(4):
+                nc.sync.dma_start(plane[32 * quad + row0:32 * quad + row0 + 4, :].bitcast(I32),
+                                    scales[0, 4 * quad:4 * quad + 4, :].bitcast(I32))
+            return plane
+
+        def load_rows(name, src):
+            raw = sb.tile([P, PACK, Q], F32, name=name, tag=name)
+            nc.sync.dma_start(raw[:], src.rearrange("(p j) q -> p j q", j=PACK))
+            return raw
+
+        def load_words(name, words):
+            pool_words = sb.tile([P, T], I32, name=name, tag=name, align_bytes=64)
+            nc.sync.dma_start(pool_words[:], words[0].rearrange("p n t -> p (n t)").bitcast(I32))
+            return pool_words
+
+        q_raw = load_rows("q_raw", query)
+        key_plane = load_scale_rows("key_plane", keys_scales, 0)
+        q2_raw = load_rows("q2_raw", query2)
+        key_words = load_words("key_words", keys_words)
+        th_col = sb.tile([P, 1], F32, name="th_col")
+        nc.gpsimd.dma_start(th_col[:], th)
+        val_plane = load_scale_rows("val_plane", vals_scales, 4)
+        size_cols = sb.tile([P, PACK], F32, name="size_cols")
+        nc.sync.dma_start(size_cols[:], size.rearrange("o (p j) -> (o p) j", j=PACK))
+        val_words = load_words("val_words", vals_words)
+        g_raw = load_rows("g_raw", gout)
+        old_sb = sb.tile([P, T], F32, name="old_sb")
+        nc.sync.dma_start(old_sb[:], old)
+
+        scattered = sb.tile([P, T], F32, name="scattered")
+        nc.vector.memset(scattered[:], 0.0)
+        w = sb.tile([P, 2 + SLOTS + 2], F32, name="w")
+        nc.vector.memset(w[:, :2], -1.0)
+        miss = sb.tile([P, 2, SLOTS + 2], F32, name="miss")
+        nc.vector.memset(miss[:, 0, SLOTS:], -float(HALF))
+        nc.vector.memset(miss[:, 1, SLOTS:], 1.0)
+
+        ident = sb.tile([P, P], F32, name="ident")
+        make_identity(nc, ident[:])
+
+        def gather_scales(name, plane):
+            picked = sb.tile([P, SLOTS], U8, name=name, align_bytes=64)
+            nc.vector.tensor_copy(picked[:], plane[:].indirect(offsets[:]))
+            return picked
+
+        def gather_words(name, pool_words, h):
+            picked = sb.tile([P, HALF], U32, name=name, align_bytes=64)
+            cols = HALF // 16
+            nc.vector.tensor_copy(picked[:], pool_words[:].bitcast(U32).indirect(offsets[:, h * cols:(h + 1) * cols]))
+            return picked
+
+        def quantise(name, raws, weave):
+            n = len(raws)
+            woven = sb.tile([P, n, Q, PACK], BF16, name=name + "_bf16", tag=name + "_bf16", align_bytes=64)
+            for i, raw in enumerate(raws):
+                weave(woven[:, i].rearrange("p (c i) t -> p c t i", i=4),
+                      raw[:].rearrange("p t (c i) -> p c t i", i=4))
+            codes = sb.tile([P, n * Q], U32, name=name + "_codes", align_bytes=64)
+            plane = sb.tile([P, n * Q], U8, name=name + "_plane", align_bytes=64)
+            nc.vector.quantize_mx(out=codes[:].bitcast(FP8X4), scales=plane[:],
+                                  in_=woven[:].rearrange("p n q t -> p (n q t)"))
+            return codes, plane
+
+        key_scales = gather_scales("key_scales", key_plane)
+        q_codes, q_plane = quantise("q", [q_raw, q2_raw], nc.vector.tensor_copy)
+        neg_th = sb.tile([P, 1], F32, name="neg_th")
+        nc.vector.tensor_scalar_mul(neg_th[:], th_col[:], -1.0)
+
+
+        score = []
+        for h in range(2):
+            picked = gather_words("key_h%d" % h, key_words, h)
+            bank = ps.tile([P, 2, HALF], F32, name="score%d" % h)
+            for s in range(2):
+                nc.tensor.matmul_mx(out=bank[:, s, :], lhsT=q_codes[:, s * Q:(s + 1) * Q].bitcast(FP8X4),
+                                    lhsT_scale=q_plane[:, s * Q:(s + 1) * Q], rhs=picked[:].bitcast(FP8X4),
+                                    rhs_scale=key_scales[:, h * HALF:(h + 1) * HALF], start=True, stop=True)
+            score.append(bank)
+        val_scales = gather_scales("val_scales", val_plane)
+
+        for h in range(2):
+            nc.scalar.activation(miss[:, :, h * HALF:(h + 1) * HALF], score[h][:], ACT.Sigmoid, bias=th_col[:], scale=-1.0)
+        g_codes, g_plane = quantise("g", [g_raw], nc.scalar.copy)
+
+        size_ps = ps.tile([P, PACK, P], F32, name="size_ps")
+        for j in range(PACK):
+            nc.tensor.transpose(size_ps[:, j, :], size_cols[:, j:j + 1].to_broadcast([P, P]), ident[:])
+        late = sb.tile([P, 2 * SLOTS], F32, name="late", tag="g_raw")
+        size_row = late[:, :SLOTS]
+        nc.scalar.copy(size_row.rearrange("m (p j) -> m p j", j=PACK), size_ps[:].rearrange("m j p -> m p j"))
+        ua = late[:, SLOTS:]
+        for h in range(2):
+            nc.scalar.activation(ua[:, h * HALF:(h + 1) * HALF], score[h][:, 0, :], ACT.Sigmoid, bias=neg_th[:])
+
+        c0 = []
+        for h in range(2):
+            picked = gather_words("val_h%d" % h, val_words, h)
+            bank = ps.tile([P, HALF], F32, name="c0_%d" % h)
+            nc.tensor.matmul_mx(out=bank[:], lhsT=g_codes[:].bitcast(FP8X4), lhsT_scale=g_plane[:],
+                                rhs=picked[:].bitcast(FP8X4), rhs_scale=val_scales[4:P, h * HALF:(h + 1) * HALF],
+                                start=True, stop=True)
+            c0.append(bank)
+
+        neg_z = sb.tile([P, 1], F32, name="neg_z", tag="g_bf16", align_bytes=64)
+        nc.vector.scalar_tensor_tensor(w[:, 2:], miss[:, 0, :], 1.0, miss[:, 1, :],
+                                       ALU.mult, ALU.mult, accum_out=neg_z[:])
+        cs = sb.tile([P, 2 + SLOTS], F32, name="cs")
+        for h in range(2):
+            nc.vector.scalar_tensor_tensor(cs[:, 2 + h * HALF:2 + (h + 1) * HALF], c0[h][:], 512.0,
+                                           size_row[:, h * HALF:(h + 1) * HALF], ALU.mult, ALU.mult,
+                                           accum_out=cs[:, h:h + 1])
+        neg_rz = sb.tile([P, 1], F32, name="neg_rz")
+        nc.vector.reciprocal(neg_rz[:], neg_z[:])
+        wn = sb.tile([P, SLOTS], F32, name="wn")
+        nc.scalar.activation(wn[:], w[:, 2:2 + SLOTS], ACT.Copy, scale=neg_rz[:])
+        uan = sb.tile([P, SLOTS], F32, name="uan")
+        nc.scalar.activation(uan[:], ua, ACT.Copy, scale=neg_rz[:])
+        y = sb.tile([P, 2 + SLOTS], F32, name="y")
+        neg_s = sb.tile([P, 1], F32, name="neg_s")
+        nc.vector.scalar_tensor_tensor(y[:], cs[:], 1.0, w[:, :2 + SLOTS], ALU.mult, ALU.mult, accum_out=neg_s[:])
+        centred = sb.tile([P, SLOTS], F32, name="centred")
+        for h in range(2):
+            nc.vector.scalar_tensor_tensor(centred[:, h * HALF:(h + 1) * HALF], wn[:, h * HALF:(h + 1) * HALF], neg_s[:],
+                                           y[:, 2 + h * HALF:2 + (h + 1) * HALF], ALU.mult, ALU.subtract)
+        for h in range(2):
+            nc.vector.tensor_tensor(scattered[:].indirect(offsets[:, h * HALF // 16:(h + 1) * HALF // 16]),
+                                    centred[:, h * HALF:(h + 1) * HALF], uan[:, h * HALF:(h + 1) * HALF], ALU.mult)
+
+        start = 0
+        for k, width in enumerate(OUT_WIDTHS):
+            cols = slice(start, start + width)
+            total = sb.tile([P, width], F32, name="total%d" % k)
+            nc.vector.tensor_tensor(total[:], scattered[:, cols], old_sb[:, cols], ALU.add)
+            nc.sync.dma_start(out[:, cols], total[:])
+            start += width

@@ -18,7 +18,7 @@ PACK = 4
 T, SLOTS, Q = 2048, 512, 128
 HALF = SLOTS // 2
 FLOPS = 3 * 2 * 512 * Q * SLOTS
-OUT_WIDTHS = [256, 512, 512, 512, 256]
+OUT_WIDTHS = [512, 512, 512, 512]
 
 
 def tile_attend_beitherquestion_s_kernel(tc, query, query2, keys_words, keys_scales, th, gout,
@@ -32,11 +32,10 @@ def tile_attend_beitherquestion_s_kernel(tc, query, query2, keys_words, keys_sca
         nc.sync.dma_start(offsets[:], offs)
 
         def load_scale_rows(name, scales, row0):
-            plane = sb.tile([P, T], U8, name=name, align_bytes=64)
+            plane = sb.tile([P, T], U8, name=name, tag=name, align_bytes=64)
             nc.vector.memset(plane[:].bitcast(I32), 0)
-            for quad in range(4):
-                nc.sync.dma_start(plane[32 * quad + row0:32 * quad + row0 + 4, :].bitcast(I32),
-                                    scales[0, 4 * quad:4 * quad + 4, :].bitcast(I32))
+            for r in range(4):
+                nc.sync.dma_start(plane[row0 + r:P:32, :].bitcast(I32), scales[0, r:16:4, :].bitcast(I32))
             return plane
 
         def load_rows(name, src):
@@ -99,8 +98,10 @@ def tile_attend_beitherquestion_s_kernel(tc, query, query2, keys_words, keys_sca
 
         key_scales = gather_scales("key_scales", key_plane)
         q_codes, q_plane = quantise("q", [q_raw, q2_raw], nc.vector.tensor_copy)
-        neg_th = sb.tile([P, 1], F32, name="neg_th")
+        neg_th = sb.tile([P, 1], F32, name="neg_th", tag="key_plane", align_bytes=64)
         nc.vector.tensor_scalar_mul(neg_th[:], th_col[:], -1.0)
+        pos_th = sb.tile([P, 1], F32, name="pos_th", tag="q_bf16", align_bytes=64)
+        nc.vector.tensor_copy(pos_th[:], th_col[:])
 
 
         score = []
@@ -115,7 +116,7 @@ def tile_attend_beitherquestion_s_kernel(tc, query, query2, keys_words, keys_sca
         val_scales = gather_scales("val_scales", val_plane)
 
         for h in range(2):
-            nc.scalar.activation(miss[:, :, h * HALF:(h + 1) * HALF], score[h][:], ACT.Sigmoid, bias=th_col[:], scale=-1.0)
+            nc.scalar.activation(miss[:, :, h * HALF:(h + 1) * HALF], score[h][:], ACT.Sigmoid, bias=pos_th[:], scale=-1.0)
         g_codes, g_plane = quantise("g", [g_raw], nc.scalar.copy)
 
         size_ps = ps.tile([P, PACK, P], F32, name="size_ps")
@@ -141,26 +142,31 @@ def tile_attend_beitherquestion_s_kernel(tc, query, query2, keys_words, keys_sca
         nc.vector.scalar_tensor_tensor(w[:, 2:], miss[:, 0, :], 1.0, miss[:, 1, :],
                                        ALU.mult, ALU.mult, accum_out=neg_z[:])
         cs = sb.tile([P, 2 + SLOTS], F32, name="cs")
-        for h in range(2):
-            nc.vector.scalar_tensor_tensor(cs[:, 2 + h * HALF:2 + (h + 1) * HALF], c0[h][:], 512.0,
-                                           size_row[:, h * HALF:(h + 1) * HALF], ALU.mult, ALU.mult,
-                                           accum_out=cs[:, h:h + 1])
         neg_rz = sb.tile([P, 1], F32, name="neg_rz")
+        slope = sb.tile([P, SLOTS], F32, name="slope")
+        halves = [slice(h * HALF, (h + 1) * HALF) for h in range(2)]
+        shifted = [slice(2 + h * HALF, 2 + (h + 1) * HALF) for h in range(2)]
+
+        def scaled_values(h):
+            nc.vector.scalar_tensor_tensor(cs[:, shifted[h]], c0[h][:], 512.0, size_row[:, halves[h]], ALU.mult, ALU.mult,
+                                           accum_out=cs[:, h:h + 1])
+
+        def slopes(h):
+            nc.vector.scalar_tensor_tensor(slope[:, halves[h]], w[:, shifted[h]], neg_rz[:], ua[:, halves[h]], ALU.mult, ALU.mult)
+
+        scaled_values(0)
         nc.vector.reciprocal(neg_rz[:], neg_z[:])
-        wn = sb.tile([P, SLOTS], F32, name="wn")
-        nc.scalar.activation(wn[:], w[:, 2:2 + SLOTS], ACT.Copy, scale=neg_rz[:])
-        uan = sb.tile([P, SLOTS], F32, name="uan")
-        nc.scalar.activation(uan[:], ua, ACT.Copy, scale=neg_rz[:])
-        y = sb.tile([P, 2 + SLOTS], F32, name="y")
-        neg_s = sb.tile([P, 1], F32, name="neg_s")
-        nc.vector.scalar_tensor_tensor(y[:], cs[:], 1.0, w[:, :2 + SLOTS], ALU.mult, ALU.mult, accum_out=neg_s[:])
+        scaled_values(1)
+        slopes(0)
+        terms = sb.tile([P, 2 + SLOTS], F32, name="terms")
+        mean = sb.tile([P, 1], F32, name="mean")
+        nc.vector.scalar_tensor_tensor(terms[:], cs[:], neg_rz[:], w[:, :2 + SLOTS], ALU.mult, ALU.mult, accum_out=mean[:])
+        slopes(1)
         centred = sb.tile([P, SLOTS], F32, name="centred")
         for h in range(2):
-            nc.vector.scalar_tensor_tensor(centred[:, h * HALF:(h + 1) * HALF], wn[:, h * HALF:(h + 1) * HALF], neg_s[:],
-                                           y[:, 2 + h * HALF:2 + (h + 1) * HALF], ALU.mult, ALU.subtract)
-        for h in range(2):
+            nc.scalar.activation(centred[:, halves[h]], cs[:, shifted[h]], ACT.Identity, bias=mean[:], scale=-1.0)
             nc.vector.tensor_tensor(scattered[:].indirect(offsets[:, h * HALF // 16:(h + 1) * HALF // 16]),
-                                    centred[:, h * HALF:(h + 1) * HALF], uan[:, h * HALF:(h + 1) * HALF], ALU.mult)
+                                    centred[:, halves[h]], slope[:, halves[h]], ALU.mult)
 
         start = 0
         for k, width in enumerate(OUT_WIDTHS):

@@ -53,10 +53,10 @@ def tile_attend_beitherquestion_s_kernel(tc, query, query2, keys_words, keys_sca
         q2_raw = load_rows("q2_raw", query2)
         key_words = load_words("key_words", keys_words)
         th_col = sb.tile([P, 1], F32, name="th_col")
-        nc.gpsimd.dma_start(th_col[:], th)
+        nc.sync.dma_start(th_col[:], th)
         val_plane = load_scale_rows("val_plane", vals_scales, 4)
         size_cols = sb.tile([P, PACK], F32, name="size_cols")
-        nc.sync.dma_start(size_cols[:], size.rearrange("o (p j) -> (o p) j", j=PACK))
+        nc.gpsimd.dma_start(size_cols[:], size.rearrange("o (p j) -> (o p) j", j=PACK))
         val_words = load_words("val_words", vals_words)
         g_raw = load_rows("g_raw", gout)
         old_sb = sb.tile([P, T], F32, name="old_sb")
@@ -98,10 +98,6 @@ def tile_attend_beitherquestion_s_kernel(tc, query, query2, keys_words, keys_sca
 
         key_scales = gather_scales("key_scales", key_plane)
         q_codes, q_plane = quantise("q", [q_raw, q2_raw], nc.vector.tensor_copy)
-        neg_th = sb.tile([P, 1], F32, name="neg_th", tag="key_plane", align_bytes=64)
-        nc.vector.tensor_scalar_mul(neg_th[:], th_col[:], -1.0)
-        pos_th = sb.tile([P, 1], F32, name="pos_th", tag="q_bf16", align_bytes=64)
-        nc.vector.tensor_copy(pos_th[:], th_col[:])
 
 
         score = []
@@ -113,10 +109,12 @@ def tile_attend_beitherquestion_s_kernel(tc, query, query2, keys_words, keys_sca
                                     lhsT_scale=q_plane[:, s * Q:(s + 1) * Q], rhs=picked[:].bitcast(FP8X4),
                                     rhs_scale=key_scales[:, h * HALF:(h + 1) * HALF], start=True, stop=True)
             score.append(bank)
+        neg_th = sb.tile([P, 1], F32, name="neg_th", tag="key_words", align_bytes=64)
+        nc.vector.tensor_scalar_mul(neg_th[:], th_col[:], -1.0)
         val_scales = gather_scales("val_scales", val_plane)
 
         for h in range(2):
-            nc.scalar.activation(miss[:, :, h * HALF:(h + 1) * HALF], score[h][:], ACT.Sigmoid, bias=pos_th[:], scale=-1.0)
+            nc.scalar.activation(miss[:, :, h * HALF:(h + 1) * HALF], score[h][:], ACT.Sigmoid, bias=th_col[:], scale=-1.0)
         g_codes, g_plane = quantise("g", [g_raw], nc.scalar.copy)
 
         size_ps = ps.tile([P, PACK, P], F32, name="size_ps")
@@ -163,10 +161,9 @@ def tile_attend_beitherquestion_s_kernel(tc, query, query2, keys_words, keys_sca
         nc.vector.scalar_tensor_tensor(terms[:], cs[:], neg_rz[:], w[:, :2 + SLOTS], ALU.mult, ALU.mult, accum_out=mean[:])
         slopes(1)
         centred = sb.tile([P, SLOTS], F32, name="centred")
-        for h in range(2):
-            nc.scalar.activation(centred[:, halves[h]], cs[:, shifted[h]], ACT.Identity, bias=mean[:], scale=-1.0)
-            nc.vector.tensor_tensor(scattered[:].indirect(offsets[:, h * HALF // 16:(h + 1) * HALF // 16]),
-                                    centred[:, halves[h]], slope[:, halves[h]], ALU.mult)
+        nc.scalar.activation(centred[:, halves[0]], cs[:, shifted[0]], ACT.Identity, bias=mean[:], scale=-1.0)
+        nc.vector.tensor_scalar(centred[:, halves[1]], cs[:, shifted[1]], -1.0, mean[:], ALU.mult, ALU.add)
+        nc.vector.tensor_tensor(scattered[:].indirect(offsets[:]), centred[:], slope[:], ALU.mult)
 
         start = 0
         for k, width in enumerate(OUT_WIDTHS):

@@ -15,15 +15,23 @@ ACT = mybir.ActivationFunctionType
 
 P = 128
 PACK = 4
+FEATURES = P * PACK
+BLOCKS = FEATURES // 32
 T, SLOTS, Q = 2048, 512, 128
 HALF = SLOTS // 2
-FLOPS = 3 * 2 * 512 * Q * SLOTS
-OUT_WIDTHS = [512, 512, 512, 512]
+GRAD_SCALE = 512.0
+EXTRA = 2
+VAL_ROW0 = 4
+OUT_WIDTH = 512
+FLOPS = 3 * 2 * FEATURES * Q * SLOTS
 
 
 def tile_attend_beitherquestion_s_kernel(tc, query, query2, keys_words, keys_scales, th, gout,
                                           vals_words, vals_scales, size, old, offs, out):
     nc = tc.nc
+    halves = [slice(h * HALF, (h + 1) * HALF) for h in range(2)]
+    shifted = [slice(EXTRA + h * HALF, EXTRA + (h + 1) * HALF) for h in range(2)]
+
     with ExitStack() as ctx:
         sb = ctx.enter_context(tc.tile_pool(name="sb", bufs=1))
         ps = ctx.enter_context(tc.psum_pool(name="ps", bufs=1))
@@ -31,11 +39,11 @@ def tile_attend_beitherquestion_s_kernel(tc, query, query2, keys_words, keys_sca
         offsets = sb.tile([P, SLOTS // 16], U16, name="offsets")
         nc.sync.dma_start(offsets[:], offs)
 
-        def load_scale_rows(name, scales, row0):
+        def load_plane(name, scales, row0):
             plane = sb.tile([P, T], U8, name=name, tag=name, align_bytes=64)
             nc.vector.memset(plane[:].bitcast(I32), 0)
             for r in range(4):
-                nc.sync.dma_start(plane[row0 + r:P:32, :].bitcast(I32), scales[0, r:16:4, :].bitcast(I32))
+                nc.sync.dma_start(plane[row0 + r:P:32, :].bitcast(I32), scales[0, r:BLOCKS:4, :].bitcast(I32))
             return plane
 
         def load_rows(name, src):
@@ -49,12 +57,12 @@ def tile_attend_beitherquestion_s_kernel(tc, query, query2, keys_words, keys_sca
             return pool_words
 
         q_raw = load_rows("q_raw", query)
-        key_plane = load_scale_rows("key_plane", keys_scales, 0)
+        key_plane = load_plane("key_plane", keys_scales, 0)
         q2_raw = load_rows("q2_raw", query2)
         key_words = load_words("key_words", keys_words)
         th_col = sb.tile([P, 1], F32, name="th_col")
         nc.sync.dma_start(th_col[:], th)
-        val_plane = load_scale_rows("val_plane", vals_scales, 4)
+        val_plane = load_plane("val_plane", vals_scales, VAL_ROW0)
         size_cols = sb.tile([P, PACK], F32, name="size_cols")
         nc.gpsimd.dma_start(size_cols[:], size.rearrange("o (p j) -> (o p) j", j=PACK))
         val_words = load_words("val_words", vals_words)
@@ -64,10 +72,10 @@ def tile_attend_beitherquestion_s_kernel(tc, query, query2, keys_words, keys_sca
 
         scattered = sb.tile([P, T], F32, name="scattered")
         nc.vector.memset(scattered[:], 0.0)
-        w = sb.tile([P, 2 + SLOTS + 2], F32, name="w")
-        nc.vector.memset(w[:, :2], -1.0)
-        miss = sb.tile([P, 2, SLOTS + 2], F32, name="miss")
-        nc.vector.memset(miss[:, 0, SLOTS:], -float(HALF))
+        w = sb.tile([P, EXTRA + SLOTS + EXTRA], F32, name="w")
+        nc.vector.memset(w[:, :EXTRA], -1.0)
+        miss = sb.tile([P, 2, SLOTS + EXTRA], F32, name="miss")
+        nc.vector.memset(miss[:, 0, SLOTS:], -float(SLOTS // EXTRA))
         nc.vector.memset(miss[:, 1, SLOTS:], 1.0)
 
         ident = sb.tile([P, P], F32, name="ident")
@@ -99,7 +107,6 @@ def tile_attend_beitherquestion_s_kernel(tc, query, query2, keys_words, keys_sca
         key_scales = gather_scales("key_scales", key_plane)
         q_codes, q_plane = quantise("q", [q_raw, q2_raw], nc.vector.tensor_copy)
 
-
         score = []
         for h in range(2):
             picked = gather_words("key_h%d" % h, key_words, h)
@@ -107,68 +114,66 @@ def tile_attend_beitherquestion_s_kernel(tc, query, query2, keys_words, keys_sca
             for s in range(2):
                 nc.tensor.matmul_mx(out=bank[:, s, :], lhsT=q_codes[:, s * Q:(s + 1) * Q].bitcast(FP8X4),
                                     lhsT_scale=q_plane[:, s * Q:(s + 1) * Q], rhs=picked[:].bitcast(FP8X4),
-                                    rhs_scale=key_scales[:, h * HALF:(h + 1) * HALF], start=True, stop=True)
+                                    rhs_scale=key_scales[:, halves[h]], start=True, stop=True)
             score.append(bank)
-        neg_th = sb.tile([P, 1], F32, name="neg_th", tag="key_words", align_bytes=64)
-        nc.vector.tensor_scalar_mul(neg_th[:], th_col[:], -1.0)
+        neg_th = sb.tile([P, 1], F32, name="neg_th")
+        nc.gpsimd.tensor_scalar(neg_th[:], th_col[:], -1.0, 0.0, ALU.mult, ALU.add)
         val_scales = gather_scales("val_scales", val_plane)
 
         for h in range(2):
-            nc.scalar.activation(miss[:, :, h * HALF:(h + 1) * HALF], score[h][:], ACT.Sigmoid, bias=th_col[:], scale=-1.0)
+            nc.scalar.activation(miss[:, :, halves[h]], score[h][:], ACT.Sigmoid, bias=th_col[:], scale=-1.0)
         g_codes, g_plane = quantise("g", [g_raw], nc.scalar.copy)
 
         size_ps = ps.tile([P, PACK, P], F32, name="size_ps")
         for j in range(PACK):
             nc.tensor.transpose(size_ps[:, j, :], size_cols[:, j:j + 1].to_broadcast([P, P]), ident[:])
-        late = sb.tile([P, 2 * SLOTS], F32, name="late", tag="g_raw")
-        size_row = late[:, :SLOTS]
+        after_gout = sb.tile([P, 2 * SLOTS], F32, name="after_gout", tag="g_raw")
+        size_row = after_gout[:, :SLOTS]
         nc.scalar.copy(size_row.rearrange("m (p j) -> m p j", j=PACK), size_ps[:].rearrange("m j p -> m p j"))
-        ua = late[:, SLOTS:]
+        ua = after_gout[:, SLOTS:]
         for h in range(2):
-            nc.scalar.activation(ua[:, h * HALF:(h + 1) * HALF], score[h][:, 0, :], ACT.Sigmoid, bias=neg_th[:])
+            nc.scalar.activation(ua[:, halves[h]], score[h][:, 0, :], ACT.Sigmoid, bias=neg_th[:])
 
         c0 = []
         for h in range(2):
             picked = gather_words("val_h%d" % h, val_words, h)
             bank = ps.tile([P, HALF], F32, name="c0_%d" % h)
             nc.tensor.matmul_mx(out=bank[:], lhsT=g_codes[:].bitcast(FP8X4), lhsT_scale=g_plane[:],
-                                rhs=picked[:].bitcast(FP8X4), rhs_scale=val_scales[4:P, h * HALF:(h + 1) * HALF],
+                                rhs=picked[:].bitcast(FP8X4), rhs_scale=val_scales[VAL_ROW0:P, halves[h]],
                                 start=True, stop=True)
             c0.append(bank)
 
         neg_z = sb.tile([P, 1], F32, name="neg_z", tag="g_bf16", align_bytes=64)
-        nc.vector.scalar_tensor_tensor(w[:, 2:], miss[:, 0, :], 1.0, miss[:, 1, :],
+        nc.vector.scalar_tensor_tensor(w[:, EXTRA:], miss[:, 0, :], 1.0, miss[:, 1, :],
                                        ALU.mult, ALU.mult, accum_out=neg_z[:])
-        cs = sb.tile([P, 2 + SLOTS], F32, name="cs")
+        cs = sb.tile([P, EXTRA + SLOTS], F32, name="cs")
         neg_rz = sb.tile([P, 1], F32, name="neg_rz")
-        slope = sb.tile([P, SLOTS], F32, name="slope")
-        halves = [slice(h * HALF, (h + 1) * HALF) for h in range(2)]
-        shifted = [slice(2 + h * HALF, 2 + (h + 1) * HALF) for h in range(2)]
+        neg_slope = sb.tile([P, SLOTS], F32, name="neg_slope")
 
-        def scaled_values(h):
-            nc.vector.scalar_tensor_tensor(cs[:, shifted[h]], c0[h][:], 512.0, size_row[:, halves[h]], ALU.mult, ALU.mult,
-                                           accum_out=cs[:, h:h + 1])
+        def make_cs(h):
+            nc.vector.scalar_tensor_tensor(cs[:, shifted[h]], c0[h][:], GRAD_SCALE, size_row[:, halves[h]],
+                                           ALU.mult, ALU.mult, accum_out=cs[:, h:h + 1])
 
-        def slopes(h):
-            nc.vector.scalar_tensor_tensor(slope[:, halves[h]], w[:, shifted[h]], neg_rz[:], ua[:, halves[h]], ALU.mult, ALU.mult)
+        def make_neg_slope(h):
+            nc.vector.scalar_tensor_tensor(neg_slope[:, halves[h]], w[:, shifted[h]], neg_rz[:], ua[:, halves[h]],
+                                           ALU.mult, ALU.mult)
 
-        scaled_values(0)
+        make_cs(0)
         nc.vector.reciprocal(neg_rz[:], neg_z[:])
-        scaled_values(1)
-        slopes(0)
-        terms = sb.tile([P, 2 + SLOTS], F32, name="terms")
+        make_cs(1)
+        make_neg_slope(0)
+        terms = sb.tile([P, EXTRA + SLOTS], F32, name="terms")
         mean = sb.tile([P, 1], F32, name="mean")
-        nc.vector.scalar_tensor_tensor(terms[:], cs[:], neg_rz[:], w[:, :2 + SLOTS], ALU.mult, ALU.mult, accum_out=mean[:])
-        slopes(1)
-        centred = sb.tile([P, SLOTS], F32, name="centred")
-        nc.scalar.activation(centred[:, halves[0]], cs[:, shifted[0]], ACT.Identity, bias=mean[:], scale=-1.0)
-        nc.vector.tensor_scalar(centred[:, halves[1]], cs[:, shifted[1]], -1.0, mean[:], ALU.mult, ALU.add)
-        nc.vector.tensor_tensor(scattered[:].indirect(offsets[:]), centred[:], slope[:], ALU.mult)
+        nc.vector.scalar_tensor_tensor(terms[:], cs[:], neg_rz[:], w[:, :EXTRA + SLOTS], ALU.mult, ALU.mult,
+                                       accum_out=mean[:])
+        make_neg_slope(1)
+        neg_centred = sb.tile([P, SLOTS], F32, name="neg_centred")
+        nc.scalar.activation(neg_centred[:, halves[0]], cs[:, shifted[0]], ACT.Identity, bias=mean[:], scale=-1.0)
+        nc.vector.tensor_scalar(neg_centred[:, halves[1]], cs[:, shifted[1]], -1.0, mean[:], ALU.mult, ALU.add)
+        nc.vector.tensor_tensor(scattered[:].indirect(offsets[:]), neg_centred[:], neg_slope[:], ALU.mult)
 
-        start = 0
-        for k, width in enumerate(OUT_WIDTHS):
-            cols = slice(start, start + width)
-            total = sb.tile([P, width], F32, name="total%d" % k)
+        for start in range(0, T, OUT_WIDTH):
+            cols = slice(start, start + OUT_WIDTH)
+            total = sb.tile([P, OUT_WIDTH], F32, name="total%d" % start)
             nc.vector.tensor_tensor(total[:], scattered[:, cols], old_sb[:, cols], ALU.add)
             nc.sync.dma_start(out[:, cols], total[:])
-            start += width

from contextlib import ExitStack

import concourse.mybir as mybir
from concourse.masks import make_identity

F32 = mybir.dt.float32
BF16 = mybir.dt.bfloat16
I32 = mybir.dt.int32
U32 = mybir.dt.uint32
U16 = mybir.dt.uint16
U8 = mybir.dt.uint8
FP8X4 = mybir.dt.float8_e4m3fn_x4
ALU = mybir.AluOpType
ACT = mybir.ActivationFunctionType

P = 128
PACK = 4
FEATURES = P * PACK
BLOCKS = FEATURES // 32
T, SLOTS, Q = 2048, 512, 128
HALF = SLOTS // 2
GRAD_SCALE = 512.0
EXTRA = 2
VAL_ROW0 = 4
OUT_WIDTH = 512
FLOPS = 3 * 2 * FEATURES * Q * SLOTS


def tile_attend_beitherquestion_s_kernel(tc, query, query2, keys_words, keys_scales, th, gout,
                                          vals_words, vals_scales, size, old, offs, out):
    nc = tc.nc
    halves = [slice(h * HALF, (h + 1) * HALF) for h in range(2)]
    shifted = [slice(EXTRA + h * HALF, EXTRA + (h + 1) * HALF) for h in range(2)]

    with ExitStack() as ctx:
        sb = ctx.enter_context(tc.tile_pool(name="sb", bufs=1))
        ps = ctx.enter_context(tc.psum_pool(name="ps", bufs=1))

        offsets = sb.tile([P, SLOTS // 16], U16, name="offsets")
        nc.sync.dma_start(offsets[:], offs)

        def load_plane(name, scales, row0):
            plane = sb.tile([P, T], U8, name=name, tag=name, align_bytes=64)
            nc.vector.memset(plane[:].bitcast(I32), 0)
            for r in range(4):
                nc.sync.dma_start(plane[row0 + r:P:32, :].bitcast(I32), scales[0, r:BLOCKS:4, :].bitcast(I32))
            return plane

        def load_rows(name, src):
            raw = sb.tile([P, PACK, Q], F32, name=name, tag=name)
            nc.sync.dma_start(raw[:], src.rearrange("(p j) q -> p j q", j=PACK))
            return raw

        def load_words(name, words):
            pool_words = sb.tile([P, T], I32, name=name, tag=name, align_bytes=64)
            nc.sync.dma_start(pool_words[:], words[0].rearrange("p n t -> p (n t)").bitcast(I32))
            return pool_words

        q_raw = load_rows("q_raw", query)
        key_plane = load_plane("key_plane", keys_scales, 0)
        q2_raw = load_rows("q2_raw", query2)
        key_words = load_words("key_words", keys_words)
        th_col = sb.tile([P, 1], F32, name="th_col")
        nc.sync.dma_start(th_col[:], th)
        val_plane = load_plane("val_plane", vals_scales, VAL_ROW0)
        size_cols = sb.tile([P, PACK], F32, name="size_cols")
        nc.gpsimd.dma_start(size_cols[:], size.rearrange("o (p j) -> (o p) j", j=PACK))
        val_words = load_words("val_words", vals_words)
        g_raw = load_rows("g_raw", gout)
        old_sb = sb.tile([P, T], F32, name="old_sb")
        nc.sync.dma_start(old_sb[:], old)

        scattered = sb.tile([P, T], F32, name="scattered")
        nc.vector.memset(scattered[:], 0.0)
        w = sb.tile([P, EXTRA + SLOTS + EXTRA], F32, name="w")
        nc.vector.memset(w[:, :EXTRA], -1.0)
        miss = sb.tile([P, 2, SLOTS + EXTRA], F32, name="miss")
        nc.vector.memset(miss[:, 0, SLOTS:], -float(SLOTS // EXTRA))
        nc.vector.memset(miss[:, 1, SLOTS:], 1.0)

        ident = sb.tile([P, P], F32, name="ident")
        make_identity(nc, ident[:])

        def gather_scales(name, plane):
            picked = sb.tile([P, SLOTS], U8, name=name, align_bytes=64)
            nc.vector.tensor_copy(picked[:], plane[:].indirect(offsets[:]))
            return picked

        def gather_words(name, pool_words, h):
            picked = sb.tile([P, HALF], U32, name=name, align_bytes=64)
            cols = HALF // 16
            nc.vector.tensor_copy(picked[:], pool_words[:].bitcast(U32).indirect(offsets[:, h * cols:(h + 1) * cols]))
            return picked

        def quantise(name, raws, weave):
            n = len(raws)
            woven = sb.tile([P, n, Q, PACK], BF16, name=name + "_bf16", tag=name + "_bf16", align_bytes=64)
            for i, raw in enumerate(raws):
                weave(woven[:, i].rearrange("p (c i) t -> p c t i", i=4),
                      raw[:].rearrange("p t (c i) -> p c t i", i=4))
            codes = sb.tile([P, n * Q], U32, name=name + "_codes", align_bytes=64)
            plane = sb.tile([P, n * Q], U8, name=name + "_plane", align_bytes=64)
            nc.vector.quantize_mx(out=codes[:].bitcast(FP8X4), scales=plane[:],
                                  in_=woven[:].rearrange("p n q t -> p (n q t)"))
            return codes, plane

        key_scales = gather_scales("key_scales", key_plane)
        q_codes, q_plane = quantise("q", [q_raw, q2_raw], nc.vector.tensor_copy)

        score = []
        for h in range(2):
            picked = gather_words("key_h%d" % h, key_words, h)
            bank = ps.tile([P, 2, HALF], F32, name="score%d" % h)
            for s in range(2):
                nc.tensor.matmul_mx(out=bank[:, s, :], lhsT=q_codes[:, s * Q:(s + 1) * Q].bitcast(FP8X4),
                                    lhsT_scale=q_plane[:, s * Q:(s + 1) * Q], rhs=picked[:].bitcast(FP8X4),
                                    rhs_scale=key_scales[:, halves[h]], start=True, stop=True)
            score.append(bank)
        neg_th = sb.tile([P, 1], F32, name="neg_th")
        nc.gpsimd.tensor_scalar(neg_th[:], th_col[:], -1.0, 0.0, ALU.mult, ALU.add)
        val_scales = gather_scales("val_scales", val_plane)

        for h in range(2):
            nc.scalar.activation(miss[:, :, halves[h]], score[h][:], ACT.Sigmoid, bias=th_col[:], scale=-1.0)
        g_codes, g_plane = quantise("g", [g_raw], nc.scalar.copy)

        size_ps = ps.tile([P, PACK, P], F32, name="size_ps")
        for j in range(PACK):
            nc.tensor.transpose(size_ps[:, j, :], size_cols[:, j:j + 1].to_broadcast([P, P]), ident[:])
        after_gout = sb.tile([P, 2 * SLOTS], F32, name="after_gout", tag="g_raw")
        size_row = after_gout[:, :SLOTS]
        nc.scalar.copy(size_row.rearrange("m (p j) -> m p j", j=PACK), size_ps[:].rearrange("m j p -> m p j"))
        ua = after_gout[:, SLOTS:]
        for h in range(2):
            nc.scalar.activation(ua[:, halves[h]], score[h][:, 0, :], ACT.Sigmoid, bias=neg_th[:])

        c0 = []
        for h in range(2):
            picked = gather_words("val_h%d" % h, val_words, h)
            bank = ps.tile([P, HALF], F32, name="c0_%d" % h)
            nc.tensor.matmul_mx(out=bank[:], lhsT=g_codes[:].bitcast(FP8X4), lhsT_scale=g_plane[:],
                                rhs=picked[:].bitcast(FP8X4), rhs_scale=val_scales[VAL_ROW0:P, halves[h]],
                                start=True, stop=True)
            c0.append(bank)

        neg_z = sb.tile([P, 1], F32, name="neg_z", tag="g_bf16", align_bytes=64)
        nc.vector.scalar_tensor_tensor(w[:, EXTRA:], miss[:, 0, :], 1.0, miss[:, 1, :],
                                       ALU.mult, ALU.mult, accum_out=neg_z[:])
        cs = sb.tile([P, EXTRA + SLOTS], F32, name="cs")
        neg_rz = sb.tile([P, 1], F32, name="neg_rz")
        neg_slope = sb.tile([P, SLOTS], F32, name="neg_slope")

        def make_cs(h):
            nc.vector.scalar_tensor_tensor(cs[:, shifted[h]], c0[h][:], GRAD_SCALE, size_row[:, halves[h]],
                                           ALU.mult, ALU.mult, accum_out=cs[:, h:h + 1])

        def make_neg_slope(h):
            nc.vector.scalar_tensor_tensor(neg_slope[:, halves[h]], w[:, shifted[h]], neg_rz[:], ua[:, halves[h]],
                                           ALU.mult, ALU.mult)

        make_cs(0)
        nc.vector.reciprocal(neg_rz[:], neg_z[:])
        make_cs(1)
        make_neg_slope(0)
        terms = sb.tile([P, EXTRA + SLOTS], F32, name="terms")
        mean = sb.tile([P, 1], F32, name="mean")
        nc.vector.scalar_tensor_tensor(terms[:], cs[:], neg_rz[:], w[:, :EXTRA + SLOTS], ALU.mult, ALU.mult,
                                       accum_out=mean[:])
        make_neg_slope(1)
        neg_centred = sb.tile([P, SLOTS], F32, name="neg_centred")
        nc.scalar.activation(neg_centred[:, halves[0]], cs[:, shifted[0]], ACT.Identity, bias=mean[:], scale=-1.0)
        nc.vector.tensor_scalar(neg_centred[:, halves[1]], cs[:, shifted[1]], -1.0, mean[:], ALU.mult, ALU.add)
        nc.vector.tensor_tensor(scattered[:].indirect(offsets[:]), neg_centred[:], neg_slope[:], ALU.mult)

        for start in range(0, T, OUT_WIDTH):
            cols = slice(start, start + OUT_WIDTH)
            total = sb.tile([P, OUT_WIDTH], F32, name="total%d" % start)
            nc.vector.tensor_tensor(total[:], scattered[:, cols], old_sb[:, cols], ALU.add)
            nc.sync.dma_start(out[:, cols], total[:])
